import numpy as np
import ml_dtypes


def mxq(x, axis, fmt="e4m3"):
    dtype, down = {"e4m3": (ml_dtypes.float8_e4m3fn, 7), "e5m2": (ml_dtypes.float8_e5m2, 14)}[fmt]
    v = np.moveaxis(np.asarray(x, np.float32).astype(ml_dtypes.bfloat16).astype(np.float64), axis, -1)
    blocks = v.reshape(v.shape[:-1] + (-1, 32))
    amax = np.abs(blocks).max(-1, keepdims=True)
    byte = np.maximum(np.where(amax > 0, np.frexp(amax)[1] - 1 + 127, 0) - down, 1)
    scale = np.exp2(byte - 127.0)
    codes = (blocks / scale).astype(np.float32).astype(dtype).astype(np.float64)
    return np.moveaxis((codes * scale).reshape(v.shape), -1, axis)


WIDE = False


def mx_kscale(k):
    if not WIDE:
        return np.ones(k)
    levels = np.array([10, -10, 5, -5, 0])
    if k % 512:
        return np.exp2(np.random.permutation(np.resize(levels, k // 32))).repeat(32)
    a = np.empty((k // 512, 16))
    for p in range(k // 512):
        a[p, :8] = np.random.permutation(np.resize(levels, 8))
        for g in range(8):
            far = levels[np.abs(levels - a[p, g]) >= 10]
            a[p, g + 8] = far[np.random.randint(len(far))]
    return np.exp2(a.ravel()).repeat(32)


def f64(x):
    return np.asarray(x).astype(np.float64)


E2M1 = np.array([0.0, 0.5, 1.0, 1.5, 2.0, 3.0, 4.0, 6.0, -0.0, -0.5, -1.0, -1.5, -2.0, -3.0, -4.0, -6.0])


def pack_weight(w, fmt):
    k, n = w.shape
    w = f64(np.asarray(w, np.float32).astype(ml_dtypes.bfloat16)).reshape(k // 32, 32, n)
    amax = np.abs(w).max(1)
    if fmt == "e4m3":
        byte = np.frexp(amax)[1] - 1 + 127 - 7
    else:
        mant, ex = np.frexp(amax / 6.0)
        byte = np.where(mant > 0.5, ex, ex - 1) + 127
    byte = np.clip(np.where(amax > 0, byte, 1), 1, 254)
    scaled = (w * np.exp2(127.0 - byte)[:, None, :]).reshape(k, n).astype(np.float32)
    by_word = np.ascontiguousarray(scaled.reshape(k // 512, 128, 4, n).transpose(0, 1, 3, 2))
    if fmt == "e4m3":
        words = by_word.astype(ml_dtypes.float8_e4m3fn).view(np.uint8)
    else:
        c = by_word.astype(ml_dtypes.float4_e2m1fn).view(np.uint8) & 0xF
        words = (c[..., 0::2] | (c[..., 1::2] << 4)).reshape(k // 512, 128, 2 * n)
    return np.ascontiguousarray(words), np.ascontiguousarray(byte.astype(np.uint8).reshape(k // 512, 16, n))


def unpack_weight(words, scales, fmt):
    g, _, n = scales.shape
    words = np.ascontiguousarray(words).reshape(g, 128, n, -1)
    if fmt == "e4m3":
        vals = words.view(ml_dtypes.float8_e4m3fn).astype(np.float64)
    else:
        nib = np.empty((g, 128, n, 4), np.uint8)
        nib[..., 0::2] = words & 0xF
        nib[..., 1::2] = words >> 4
        vals = E2M1[nib]
    vals = vals * np.repeat(np.exp2(scales.astype(np.float64) - 127.0), 8, axis=1)[..., None]
    return vals.transpose(0, 1, 3, 2).reshape(g * 512, n)


def gelu(v):
    return 0.5 * v * (1.0 + np.tanh(np.sqrt(2.0 / np.pi) * (v + 0.044715 * v**3)))


K, M, T = 512, 512, 1536


def setup_inputs():
    n = np.random.standard_normal
    s = mx_kscale(K)[:, None]
    w = n((K, M)) / np.sqrt(K) / s
    w4 = pack_weight(w, "e2m1")
    rest = w - unpack_weight(*w4, "e2m1")
    p_r8 = pack_weight(rest, "e4m3")
    return {
        "x": (n((K, T)) * s).astype(np.float32),
        "w4_words": w4[0],
        "w4_scales": w4[1],
        "r8_words": p_r8[0],
        "r8_scales": p_r8[1],
        "b": (0.3 * n(512)).astype(np.float32),
    }


def reference(x, w4_words, w4_scales, r8_words, r8_scales, b):
    x_ = mxq(f64(x), 0, "e4m3")
    w4_ = unpack_weight(w4_words, w4_scales, "e2m1")
    r8_ = unpack_weight(r8_words, r8_scales, "e4m3")
    y = x_.T @ w4_ + x_.T @ r8_
    return gelu(y + f64(b)[None, :])

@@ -1,0 +1,143 @@
+from contextlib import ExitStack
+
+import concourse.mybir as mybir
+from concourse.masks import make_identity
+
+K, N, T = 512, 512, 1536
+FLOPS = 2 * 2 * K * N * T
+
+F32 = mybir.dt.float32
+BF16 = mybir.dt.bfloat16
+I32 = mybir.dt.int32
+U32 = mybir.dt.uint32
+U8 = mybir.dt.uint8
+FP8X4 = mybir.dt.float8_e4m3fn_x4
+FP4X4 = mybir.dt.float4_e2m1fn_x4
+GELU = mybir.ActivationFunctionType.Gelu_apprx_tanh
+MULT = mybir.AluOpType.mult
+ADD = mybir.AluOpType.add
+
+P = 128
+TILES = T // P
+CHUNKS = [128,256,256,256,256,256,128]
+COPY_ENGINE = "VSVSVSVSVSVS"
+
+
+def tile_mix_resid_tm_gelu_kernel(tc, x, w4_words, w4_scales, r8_words, r8_scales, b, out):
+    nc = tc.nc
+    with ExitStack() as ctx:
+        keep = ctx.enter_context(tc.tile_pool(name="keep", bufs=1))
+        psum = ctx.enter_context(tc.psum_pool(name="psum", bufs=7))
+        psum_b = ctx.enter_context(tc.psum_pool(name="psum_b", bufs=1))
+        ctx.enter_context(tc.manual_schedule())
+
+        w4_plane = keep.tile([P, N], U8, align_bytes=64, name="w4_plane")
+        r8_plane = keep.tile([P, N], U8, align_bytes=64, name="r8_plane")
+        w4 = keep.tile([P, 2 * N], U8, align_bytes=64, name="w4")
+        r8 = keep.tile([P, 4 * N], U8, align_bytes=64, name="r8")
+        warm = keep.tile([P, 1], F32, name="warm")
+        b_cols = keep.tile([P, 4], F32, name="b_cols")
+        bias = keep.tile([P, N], F32, name="bias")
+        ident = keep.tile([P, P], F32, name="ident")
+
+        xv = x.rearrange("(p j) t -> p j t", j=4)
+        raws = []
+        starts = []
+        t0 = 0
+        for i, w in enumerate(CHUNKS):
+            raw = keep.tile([P, 4, w], F32, name=f"raw{i}")
+            raws.append(raw)
+            starts.append(t0)
+            t0 += w
+
+        def load_x(i):
+            nc.sync.dma_start(out=raws[i][:], in_=xv[:, :, starts[i] : starts[i] + CHUNKS[i]])
+
+        nc.vector.memset(ident[:], 0.0)
+        nc.vector.memset(w4_plane[:].bitcast(I32), 0)
+        nc.vector.memset(r8_plane[:].bitcast(I32), 0)
+        nc.vector.memset(warm[:], 0.0)
+        nc.scalar.dma_start(out=b_cols[:], in_=b.rearrange("(p m) -> p m", m=4))
+        make_identity(nc, ident[:], nomemset=True)
+        nc.scalar.activation(out=warm[:], in_=warm[:], func=GELU)
+
+        load_x(0)
+        for q in range(4):
+            nc.sync.dma_start(out=w4_plane[32 * q : 32 * q + 4, :].bitcast(I32), in_=w4_scales[0, 4 * q : 4 * q + 4, :].bitcast(I32))
+        nc.sync.dma_start(out=w4[:].bitcast(I32), in_=w4_words[0].bitcast(I32))
+        nc.sync.dma_start(out=r8[:].bitcast(I32), in_=r8_words[0].rearrange("p n i -> p (n i)").bitcast(I32))
+        load_x(1)
+        for q in range(4):
+            nc.sync.dma_start(out=r8_plane[32 * q : 32 * q + 4, :].bitcast(I32), in_=r8_scales[0, 4 * q : 4 * q + 4, :].bitcast(I32))
+        for i in range(2, len(CHUNKS)):
+            load_x(i)
+
+        b_ps = psum_b.tile([P, 4, P], F32, name="b_ps")
+        for m in range(4):
+            nc.tensor.transpose(b_ps[:, m, :], b_cols[:, m : m + 1].to_broadcast([P, P]), ident[:])
+
+        grouped = {}
+        codes = {}
+        planes = {}
+        accs = {}
+        ys = {}
+
+        def copy(i):
+            c = max(j for j in range(len(CHUNKS)) if starts[j] <= i * P)
+            lo = i * P - starts[c]
+            g = keep.tile([P, P, 4], BF16, align_bytes=64, name=f"grouped{i}")
+            grouped[i] = g
+            dst = g[:].rearrange("p (c i) j -> p c j i", i=4)
+            src = raws[c][:, :, lo : lo + P].rearrange("p j (c i) -> p c j i", i=4)
+            e = COPY_ENGINE[i]
+            if e == "V":
+                nc.vector.tensor_copy(out=dst, in_=src)
+            elif e == "S":
+                nc.scalar.copy(out=dst, in_=src)
+            else:
+                nc.gpsimd.tensor_scalar(out=dst, in0=src, scalar1=1.0, scalar2=0.0, op0=MULT, op1=ADD)
+
+        def quantize(i):
+            cd = keep.tile([P, P], U32, align_bytes=64, name=f"codes{i}")
+            pl = keep.tile([P, P], U8, align_bytes=64, name=f"plane{i}")
+            codes[i] = cd
+            planes[i] = pl
+            nc.vector.quantize_mx(out=cd[:].bitcast(FP8X4), scales=pl[:], in_=grouped[i][:].rearrange("p w j -> p (w j)"))
+
+        def multiply(i):
+            acc = psum.tile([P, N], F32, name="acc")
+            accs[i] = acc
+            nc.tensor.matmul_mx(out=acc[:], lhsT=codes[i][:].bitcast(FP8X4), lhsT_scale=planes[i][:],
+                                rhs=w4[:].bitcast(FP4X4), rhs_scale=w4_plane[:], start=True, stop=False)
+            nc.tensor.matmul_mx(out=acc[:], lhsT=codes[i][:].bitcast(FP8X4), lhsT_scale=planes[i][:],
+                                rhs=r8[:].bitcast(FP8X4), rhs_scale=r8_plane[:], start=False, stop=True)
+
+        def add_bias(i):
+            y = keep.tile([P, N], F32, name=f"y{i}")
+            ys[i] = y
+            nc.vector.tensor_tensor(out=y[:], in0=accs[i][:], in1=bias[:], op=ADD)
+
+        def gelu_store(i):
+            o = keep.tile([P, N], F32, name=f"o{i}")
+            halves = 2 if i == TILES - 1 else 1
+            w = N // halves
+            for h in range(halves):
+                nc.scalar.activation(out=o[:, h * w : (h + 1) * w], in_=ys[i][:, h * w : (h + 1) * w], func=GELU)
+                nc.sync.dma_start(out=out[i * P : (i + 1) * P, h * w : (h + 1) * w], in_=o[:, h * w : (h + 1) * w])
+
+        copy(0)
+        quantize(0)
+        multiply(0)
+        copy(1)
+        copy(2)
+        nc.scalar.copy(out=bias[:].rearrange("t (p m) -> t p m", m=4), in_=b_ps[:].rearrange("t m p -> t p m"))
+        quantize(1)
+        multiply(1)
+        for i in range(TILES):
+            if i + 3 < TILES:
+                copy(i + 3)
+            if i + 2 < TILES:
+                quantize(i + 2)
+                multiply(i + 2)
+            add_bias(i)
+            gelu_store(i)

@@ -19,8 +19,8 @@ ADD = mybir.AluOpType.add
 
 P = 128
 TILES = T // P
-CHUNKS = [128,256,256,256,256,256,128]
-COPY_ENGINE = "VSVSVSVSVSVS"
+CHUNKS = [128,128,256,384,384,256]
+COPY_ENGINE = "VGSGSGGSGGSG"
 
 
 def tile_mix_resid_tm_gelu_kernel(tc, x, w4_words, w4_scales, r8_words, r8_scales, b, out):
@@ -53,22 +53,24 @@ def tile_mix_resid_tm_gelu_kernel(tc, x, w4_words, w4_scales, r8_words, r8_scale
         def load_x(i):
             nc.sync.dma_start(out=raws[i][:], in_=xv[:, :, starts[i] : starts[i] + CHUNKS[i]])
 
-        nc.vector.memset(ident[:], 0.0)
         nc.vector.memset(w4_plane[:].bitcast(I32), 0)
         nc.vector.memset(r8_plane[:].bitcast(I32), 0)
+        nc.vector.memset(ident[:], 0.0)
         nc.vector.memset(warm[:], 0.0)
-        nc.scalar.dma_start(out=b_cols[:], in_=b.rearrange("(p m) -> p m", m=4))
-        make_identity(nc, ident[:], nomemset=True)
         nc.scalar.activation(out=warm[:], in_=warm[:], func=GELU)
 
+        def load_scales(plane, scales):
+            for q in range(4):
+                nc.sync.dma_start(out=plane[32 * q : 32 * q + 4, :].bitcast(I32), in_=scales[0, 4 * q : 4 * q + 4, :].bitcast(I32))
+
+        nc.sync.dma_start(out=b_cols[:], in_=b.rearrange("(p m) -> p m", m=4))
+        nc.gpsimd.dma_start(out=w4[:].bitcast(I32), in_=w4_words[0].bitcast(I32))
         load_x(0)
-        for q in range(4):
-            nc.sync.dma_start(out=w4_plane[32 * q : 32 * q + 4, :].bitcast(I32), in_=w4_scales[0, 4 * q : 4 * q + 4, :].bitcast(I32))
-        nc.sync.dma_start(out=w4[:].bitcast(I32), in_=w4_words[0].bitcast(I32))
-        nc.sync.dma_start(out=r8[:].bitcast(I32), in_=r8_words[0].rearrange("p n i -> p (n i)").bitcast(I32))
+        load_scales(w4_plane, w4_scales)
         load_x(1)
-        for q in range(4):
-            nc.sync.dma_start(out=r8_plane[32 * q : 32 * q + 4, :].bitcast(I32), in_=r8_scales[0, 4 * q : 4 * q + 4, :].bitcast(I32))
+        nc.sync.dma_start(out=r8[:].bitcast(I32), in_=r8_words[0].rearrange("p n i -> p (n i)").bitcast(I32))
+        load_scales(r8_plane, r8_scales)
+        make_identity(nc, ident[:], nomemset=True)
         for i in range(2, len(CHUNKS)):
             load_x(i)
 
@@ -80,7 +82,6 @@ def tile_mix_resid_tm_gelu_kernel(tc, x, w4_words, w4_scales, r8_words, r8_scale
         codes = {}
         planes = {}
         accs = {}
-        ys = {}
 
         def copy(i):
             c = max(j for j in range(len(CHUNKS)) if starts[j] <= i * P)
@@ -112,32 +113,22 @@ def tile_mix_resid_tm_gelu_kernel(tc, x, w4_words, w4_scales, r8_words, r8_scale
             nc.tensor.matmul_mx(out=acc[:], lhsT=codes[i][:].bitcast(FP8X4), lhsT_scale=planes[i][:],
                                 rhs=r8[:].bitcast(FP8X4), rhs_scale=r8_plane[:], start=False, stop=True)
 
-        def add_bias(i):
+        def finish(i):
             y = keep.tile([P, N], F32, name=f"y{i}")
-            ys[i] = y
-            nc.vector.tensor_tensor(out=y[:], in0=accs[i][:], in1=bias[:], op=ADD)
-
-        def gelu_store(i):
             o = keep.tile([P, N], F32, name=f"o{i}")
-            halves = 2 if i == TILES - 1 else 1
-            w = N // halves
-            for h in range(halves):
-                nc.scalar.activation(out=o[:, h * w : (h + 1) * w], in_=ys[i][:, h * w : (h + 1) * w], func=GELU)
-                nc.sync.dma_start(out=out[i * P : (i + 1) * P, h * w : (h + 1) * w], in_=o[:, h * w : (h + 1) * w])
+            w = N // 2 if i == TILES - 1 else N
+            for n0 in range(0, N, w):
+                cols = slice(n0, n0 + w)
+                nc.vector.tensor_tensor(out=y[:, cols], in0=accs[i][:, cols], in1=bias[:, cols], op=ADD)
+                nc.scalar.activation(out=o[:, cols], in_=y[:, cols], func=GELU)
+                nc.sync.dma_start(out=out[i * P : (i + 1) * P, cols], in_=o[:, cols])
 
-        copy(0)
-        quantize(0)
-        multiply(0)
-        copy(1)
-        copy(2)
         nc.scalar.copy(out=bias[:].rearrange("t (p m) -> t p m", m=4), in_=b_ps[:].rearrange("t m p -> t p m"))
-        quantize(1)
-        multiply(1)
-        for i in range(TILES):
-            if i + 3 < TILES:
-                copy(i + 3)
-            if i + 2 < TILES:
+        for i in range(-4, TILES):
+            if 0 <= i + 4 < TILES:
+                copy(i + 4)
+            if 0 <= i + 2 < TILES:
                 quantize(i + 2)
                 multiply(i + 2)
-            add_bias(i)
-            gelu_store(i)
+            if i >= 0:
+                finish(i)

@@ -19,8 +19,8 @@ ADD = mybir.AluOpType.add
 
 P = 128
 TILES = T // P
-CHUNKS = [128,128,256,384,384,256]
-COPY_ENGINE = "VGSGSGGSGGSG"
+CHUNKS = [128,256,256,256,256,256,128]
+COPY_ENGINE = ["V","V","G","S","G","S","V","S","S","V","VS","G"]
 
 
 def tile_mix_resid_tm_gelu_kernel(tc, x, w4_words, w4_scales, r8_words, r8_scales, b, out):
@@ -65,12 +65,13 @@ def tile_mix_resid_tm_gelu_kernel(tc, x, w4_words, w4_scales, r8_words, r8_scale
 
         nc.sync.dma_start(out=b_cols[:], in_=b.rearrange("(p m) -> p m", m=4))
         nc.gpsimd.dma_start(out=w4[:].bitcast(I32), in_=w4_words[0].bitcast(I32))
+        make_identity(nc, ident[:], nomemset=True)
         load_x(0)
         load_scales(w4_plane, w4_scales)
         load_x(1)
         nc.sync.dma_start(out=r8[:].bitcast(I32), in_=r8_words[0].rearrange("p n i -> p (n i)").bitcast(I32))
         load_scales(r8_plane, r8_scales)
-        make_identity(nc, ident[:], nomemset=True)
+
         for i in range(2, len(CHUNKS)):
             load_x(i)
 
@@ -88,15 +89,16 @@ def tile_mix_resid_tm_gelu_kernel(tc, x, w4_words, w4_scales, r8_words, r8_scale
             lo = i * P - starts[c]
             g = keep.tile([P, P, 4], BF16, align_bytes=64, name=f"grouped{i}")
             grouped[i] = g
-            dst = g[:].rearrange("p (c i) j -> p c j i", i=4)
-            src = raws[c][:, :, lo : lo + P].rearrange("p j (c i) -> p c j i", i=4)
-            e = COPY_ENGINE[i]
-            if e == "V":
-                nc.vector.tensor_copy(out=dst, in_=src)
-            elif e == "S":
-                nc.scalar.copy(out=dst, in_=src)
-            else:
-                nc.gpsimd.tensor_scalar(out=dst, in0=src, scalar1=1.0, scalar2=0.0, op0=MULT, op1=ADD)
+            w = P // len(COPY_ENGINE[i])
+            for n, e in enumerate(COPY_ENGINE[i]):
+                dst = g[:, n * w : (n + 1) * w, :].rearrange("p (c i) j -> p c j i", i=4)
+                src = raws[c][:, :, lo + n * w : lo + (n + 1) * w].rearrange("p j (c i) -> p c j i", i=4)
+                if e == "V":
+                    nc.vector.tensor_copy(out=dst, in_=src)
+                elif e == "S":
+                    nc.scalar.copy(out=dst, in_=src)
+                else:
+                    nc.gpsimd.tensor_scalar(out=dst, in0=src, scalar1=1.0, scalar2=0.0, op0=MULT, op1=ADD)
 
         def quantize(i):
             cd = keep.tile([P, P], U32, align_bytes=64, name=f"codes{i}")
@@ -124,11 +126,16 @@ def tile_mix_resid_tm_gelu_kernel(tc, x, w4_words, w4_scales, r8_words, r8_scale
                 nc.sync.dma_start(out=out[i * P : (i + 1) * P, cols], in_=o[:, cols])
 
         nc.scalar.copy(out=bias[:].rearrange("t (p m) -> t p m", m=4), in_=b_ps[:].rearrange("t m p -> t p m"))
-        for i in range(-4, TILES):
-            if 0 <= i + 4 < TILES:
-                copy(i + 4)
-            if 0 <= i + 2 < TILES:
-                quantize(i + 2)
-                multiply(i + 2)
-            if i >= 0:
-                finish(i)
+        copied = 0
+        quantized = 0
+        for i in range(TILES):
+            while copied < min(TILES, i + 4 + 1):
+                copy(copied)
+                copied += 1
+            ready = quantized
+            ahead = 2 if i < 0 else 2
+            while quantized < min(TILES, i + ahead + 1):
+                quantize(quantized)
+                multiply(quantized)
+                quantized += 1
+            finish(i)

from contextlib import ExitStack

import concourse.mybir as mybir
from concourse.masks import make_identity

K, N, T = 512, 512, 1536
FLOPS = 2 * 2 * K * N * T

F32 = mybir.dt.float32
BF16 = mybir.dt.bfloat16
I32 = mybir.dt.int32
U32 = mybir.dt.uint32
U8 = mybir.dt.uint8
FP8X4 = mybir.dt.float8_e4m3fn_x4
FP4X4 = mybir.dt.float4_e2m1fn_x4
GELU = mybir.ActivationFunctionType.Gelu_apprx_tanh
MULT = mybir.AluOpType.mult
ADD = mybir.AluOpType.add

P = 128
TILES = T // P
CHUNKS = [128,256,256,256,256,256,128]
COPY_ENGINE = ["V","V","G","S","G","S","V","S","S","V","VS","G"]


def tile_mix_resid_tm_gelu_kernel(tc, x, w4_words, w4_scales, r8_words, r8_scales, b, out):
    nc = tc.nc
    with ExitStack() as ctx:
        keep = ctx.enter_context(tc.tile_pool(name="keep", bufs=1))
        psum = ctx.enter_context(tc.psum_pool(name="psum", bufs=7))
        psum_b = ctx.enter_context(tc.psum_pool(name="psum_b", bufs=1))
        ctx.enter_context(tc.manual_schedule())

        w4_plane = keep.tile([P, N], U8, align_bytes=64, name="w4_plane")
        r8_plane = keep.tile([P, N], U8, align_bytes=64, name="r8_plane")
        w4 = keep.tile([P, 2 * N], U8, align_bytes=64, name="w4")
        r8 = keep.tile([P, 4 * N], U8, align_bytes=64, name="r8")
        warm = keep.tile([P, 1], F32, name="warm")
        b_cols = keep.tile([P, 4], F32, name="b_cols")
        bias = keep.tile([P, N], F32, name="bias")
        ident = keep.tile([P, P], F32, name="ident")

        xv = x.rearrange("(p j) t -> p j t", j=4)
        raws = []
        starts = []
        t0 = 0
        for i, w in enumerate(CHUNKS):
            raw = keep.tile([P, 4, w], F32, name=f"raw{i}")
            raws.append(raw)
            starts.append(t0)
            t0 += w

        def load_x(i):
            nc.sync.dma_start(out=raws[i][:], in_=xv[:, :, starts[i] : starts[i] + CHUNKS[i]])

        nc.vector.memset(w4_plane[:].bitcast(I32), 0)
        nc.vector.memset(r8_plane[:].bitcast(I32), 0)
        nc.vector.memset(ident[:], 0.0)
        nc.vector.memset(warm[:], 0.0)
        nc.scalar.activation(out=warm[:], in_=warm[:], func=GELU)

        def load_scales(plane, scales):
            for q in range(4):
                nc.sync.dma_start(out=plane[32 * q : 32 * q + 4, :].bitcast(I32), in_=scales[0, 4 * q : 4 * q + 4, :].bitcast(I32))

        nc.sync.dma_start(out=b_cols[:], in_=b.rearrange("(p m) -> p m", m=4))
        nc.gpsimd.dma_start(out=w4[:].bitcast(I32), in_=w4_words[0].bitcast(I32))
        make_identity(nc, ident[:], nomemset=True)
        load_x(0)
        load_scales(w4_plane, w4_scales)
        load_x(1)
        nc.sync.dma_start(out=r8[:].bitcast(I32), in_=r8_words[0].rearrange("p n i -> p (n i)").bitcast(I32))
        load_scales(r8_plane, r8_scales)

        for i in range(2, len(CHUNKS)):
            load_x(i)

        b_ps = psum_b.tile([P, 4, P], F32, name="b_ps")
        for m in range(4):
            nc.tensor.transpose(b_ps[:, m, :], b_cols[:, m : m + 1].to_broadcast([P, P]), ident[:])

        grouped = {}
        codes = {}
        planes = {}
        accs = {}

        def copy(i):
            c = max(j for j in range(len(CHUNKS)) if starts[j] <= i * P)
            lo = i * P - starts[c]
            g = keep.tile([P, P, 4], BF16, align_bytes=64, name=f"grouped{i}")
            grouped[i] = g
            w = P // len(COPY_ENGINE[i])
            for n, e in enumerate(COPY_ENGINE[i]):
                dst = g[:, n * w : (n + 1) * w, :].rearrange("p (c i) j -> p c j i", i=4)
                src = raws[c][:, :, lo + n * w : lo + (n + 1) * w].rearrange("p j (c i) -> p c j i", i=4)
                if e == "V":
                    nc.vector.tensor_copy(out=dst, in_=src)
                elif e == "S":
                    nc.scalar.copy(out=dst, in_=src)
                else:
                    nc.gpsimd.tensor_scalar(out=dst, in0=src, scalar1=1.0, scalar2=0.0, op0=MULT, op1=ADD)

        def quantize(i):
            cd = keep.tile([P, P], U32, align_bytes=64, name=f"codes{i}")
            pl = keep.tile([P, P], U8, align_bytes=64, name=f"plane{i}")
            codes[i] = cd
            planes[i] = pl
            nc.vector.quantize_mx(out=cd[:].bitcast(FP8X4), scales=pl[:], in_=grouped[i][:].rearrange("p w j -> p (w j)"))

        def multiply(i):
            acc = psum.tile([P, N], F32, name="acc")
            accs[i] = acc
            nc.tensor.matmul_mx(out=acc[:], lhsT=codes[i][:].bitcast(FP8X4), lhsT_scale=planes[i][:],
                                rhs=w4[:].bitcast(FP4X4), rhs_scale=w4_plane[:], start=True, stop=False)
            nc.tensor.matmul_mx(out=acc[:], lhsT=codes[i][:].bitcast(FP8X4), lhsT_scale=planes[i][:],
                                rhs=r8[:].bitcast(FP8X4), rhs_scale=r8_plane[:], start=False, stop=True)

        def finish(i):
            y = keep.tile([P, N], F32, name=f"y{i}")
            o = keep.tile([P, N], F32, name=f"o{i}")
            w = N // 2 if i == TILES - 1 else N
            for n0 in range(0, N, w):
                cols = slice(n0, n0 + w)
                nc.vector.tensor_tensor(out=y[:, cols], in0=accs[i][:, cols], in1=bias[:, cols], op=ADD)
                nc.scalar.activation(out=o[:, cols], in_=y[:, cols], func=GELU)
                nc.sync.dma_start(out=out[i * P : (i + 1) * P, cols], in_=o[:, cols])

        nc.scalar.copy(out=bias[:].rearrange("t (p m) -> t p m", m=4), in_=b_ps[:].rearrange("t m p -> t p m"))
        copied = 0
        quantized = 0
        for i in range(TILES):
            while copied < min(TILES, i + 4 + 1):
                copy(copied)
                copied += 1
            ready = quantized
            ahead = 2 if i < 0 else 2
            while quantized < min(TILES, i + ahead + 1):
                quantize(quantized)
                multiply(quantized)
                quantized += 1
            finish(i)
